import numpy as np
import ml_dtypes


def mxq(x, axis, fmt="e4m3"):
    dtype, down = {"e4m3": (ml_dtypes.float8_e4m3fn, 7), "e5m2": (ml_dtypes.float8_e5m2, 14)}[fmt]
    v = np.moveaxis(np.asarray(x, np.float32).astype(ml_dtypes.bfloat16).astype(np.float64), axis, -1)
    blocks = v.reshape(v.shape[:-1] + (-1, 32))
    amax = np.abs(blocks).max(-1, keepdims=True)
    byte = np.maximum(np.where(amax > 0, np.frexp(amax)[1] - 1 + 127, 0) - down, 1)
    scale = np.exp2(byte - 127.0)
    codes = (blocks / scale).astype(np.float32).astype(dtype).astype(np.float64)
    return np.moveaxis((codes * scale).reshape(v.shape), -1, axis)


WIDE = False


def mx_kscale(k):
    if not WIDE:
        return np.ones(k)
    levels = np.array([10, -10, 5, -5, 0])
    if k % 512:
        return np.exp2(np.random.permutation(np.resize(levels, k // 32))).repeat(32)
    a = np.empty((k // 512, 16))
    for p in range(k // 512):
        a[p, :8] = np.random.permutation(np.resize(levels, 8))
        for g in range(8):
            far = levels[np.abs(levels - a[p, g]) >= 10]
            a[p, g + 8] = far[np.random.randint(len(far))]
    return np.exp2(a.ravel()).repeat(32)


def f64(x):
    return np.asarray(x).astype(np.float64)


def striped8(idx):
    return np.concatenate([x.reshape(-1, 16).T for x in idx]).astype(np.uint16)


def runs(offs, k):
    lists = np.stack([offs[16 * r : 16 * r + 16].T.reshape(-1) for r in range(8)]).astype(np.int64)
    return lists[np.arange(k) % 512 // 64]


def pack_weight(w):
    k, n = w.shape
    w = f64(np.asarray(w, np.float32).astype(ml_dtypes.bfloat16)).reshape(k // 32, 32, n)
    amax = np.abs(w).max(1)
    byte = np.clip(np.where(amax > 0, np.frexp(amax)[1] - 1 + 127 - 7, 1), 1, 254)
    scaled = (w * np.exp2(127.0 - byte)[:, None, :]).reshape(k, n).astype(np.float32)
    words = np.ascontiguousarray(scaled.reshape(k // 512, 128, 4, n).transpose(0, 1, 3, 2)).astype(ml_dtypes.float8_e4m3fn).view(np.uint8)
    return words, np.ascontiguousarray(byte.astype(np.uint8).reshape(k // 512, 16, n))


def unpack_weight(words, scales):
    g, p, n, _ = words.shape
    vals = np.ascontiguousarray(words).view(ml_dtypes.float8_e4m3fn).astype(np.float64) * np.repeat(np.exp2(scales.astype(np.float64) - 127.0), 8, axis=1)[..., None]
    return vals.transpose(0, 1, 3, 2).reshape(g * 512, n)

def planes(y):
    n, m = y.shape
    v = y.astype(np.float32).astype(ml_dtypes.bfloat16).astype(np.float64).reshape(n // 32, 32, m)
    top = np.abs(v).max(1)
    byte = np.clip(np.where(top > 0, np.frexp(top)[1] - 1 + 127 - 7, 1), 1, 254)
    codes = (v * np.exp2(127.0 - byte)[:, None, :]).reshape(n, m).astype(np.float32).astype(ml_dtypes.float8_e4m3fn).view(np.uint8)
    words = codes.reshape(n // 512, 128, 4, m).transpose(0, 1, 3, 2)
    return np.ascontiguousarray(words), np.ascontiguousarray(byte.astype(np.uint8).reshape(n // 512, 16, m))


K, T, S, N = 512, 2048, 512, 512
P = 2 ** 7


def setup_inputs():
    n = np.random.standard_normal
    s = mx_kscale(K)[:, None]
    packed_xT = pack_weight(n((K, T)) * s)
    return {
        "x_words": packed_xT[0],
        "x_scales": packed_xT[1],
        "w1": (n((K, N)) / np.sqrt(K) / s).astype(np.float32),
        "prior": np.tile(0.5 * np.random.standard_normal(S), (P, 1)).astype(np.float32),
        "offs": striped8(np.random.randint(0, T, (8, S))),
    }


def reference(x_words, x_scales, w1, prior, offs):
    xq = unpack_weight(x_words, x_scales)[np.arange(K)[:, None], runs(offs, K)]
    y = mxq(f64(w1), 0, "e4m3").T @ xq
    yp = y + f64(prior)[:1]
    e = np.exp(yp - yp.max(axis=1, keepdims=True))
    out_0 = e / e.sum(axis=1, keepdims=True)
    return (out_0,) + planes(out_0)

@@ -1,0 +1,138 @@
+from contextlib import ExitStack
+
+import concourse.mybir as mybir
+
+K, T, S, N = 512, 2048, 512, 512
+FLOPS = 2 * K * S * N
+
+F32 = mybir.dt.float32
+BF16 = mybir.dt.bfloat16
+I32 = mybir.dt.int32
+U32 = mybir.dt.uint32
+U16 = mybir.dt.uint16
+U8 = mybir.dt.uint8
+FP8X4 = mybir.dt.float8_e4m3fn_x4
+ALU = mybir.AluOpType
+ACT = mybir.ActivationFunctionType
+AX = mybir.AxisListType
+
+P = 128
+PACK = 4
+HALF = S // 2
+W_SPLIT = 80
+C_SPLIT = 384
+
+
+def tile_picked_phrank_none_po_kernel(tc, x_words, x_scales, w1, prior, offs, out_0, out_1, out_2):
+    nc = tc.nc
+    with ExitStack() as ctx:
+        keep = ctx.enter_context(tc.tile_pool(name="keep", bufs=1))
+        psum = ctx.enter_context(tc.psum_pool(name="psum", bufs=1))
+
+        offsets = keep.tile([P, S // 16], U16, name="offsets")
+        scale_table = keep.tile([P, T], U8, name="scale_table", align_bytes=64)
+        word_table = keep.tile([P, T], I32, name="word_table", align_bytes=64)
+        w_raw = keep.tile([P, PACK, N], F32, name="w_raw", align_bytes=64)
+        prior_sb = keep.tile([P, S], F32, name="prior_sb", align_bytes=64)
+        warm = keep.tile([P, 8], F32, name="warm")
+        warm_out = keep.tile([P, 8], F32, name="warm_out")
+
+        nc.sync.dma_start(offsets[:], offs)
+        nc.sync.dma_start(out=w_raw[:], in_=w1.rearrange("(p j) m -> p j m", j=PACK))
+        nc.sync.dma_start(out=word_table[:], in_=x_words[0].rearrange("p n t -> p (n t)").bitcast(I32))
+        nc.sync.dma_start(out=prior_sb[:], in_=prior)
+
+        nc.vector.memset(scale_table[:].bitcast(I32), 0)
+        nc.vector.memset(warm[:], 0.0)
+        scale_rows = x_scales[0].bitcast(I32).rearrange("(r i) n -> i r n", i=2)
+        for i in range(2):
+            nc.scalar.dma_start(out=scale_table[:].bitcast(I32)[i:P:16, :], in_=scale_rows[i])
+        nc.scalar.activation(warm_out[:], warm[:], ACT.Exp)
+
+        picked_scales = keep.tile([P, S], U8, name="picked_scales", align_bytes=64)
+        nc.vector.tensor_copy(picked_scales[:], scale_table[:].indirect(offsets[:]))
+        x_plane = keep.tile([P, S], U8, name="x_plane", align_bytes=64)
+        nc.vector.tensor_copy(x_plane[:].bitcast(I32), picked_scales[:].bitcast(I32))
+        for i in range(2):
+            nc.scalar.dma_start(out=x_plane[:].bitcast(I32)[2 + i : P : 32, :], in_=picked_scales[:].bitcast(I32)[16 + i : P : 32, :])
+
+        w_grouped = keep.tile([P, PACK, P, PACK], BF16, name="w_grouped", align_bytes=64)
+        w_dst = w_grouped[:].rearrange("p t m j -> p m t j")
+        w_src = w_raw[:].rearrange("p j (m t) -> p m t j", t=PACK)
+        nc.vector.tensor_copy(out=w_dst[:, :W_SPLIT], in_=w_src[:, :W_SPLIT])
+        nc.scalar.copy(out=w_dst[:, W_SPLIT:], in_=w_src[:, W_SPLIT:])
+        w_codes = keep.tile([P, N], U32, name="w_codes", align_bytes=64)
+        w_plane = keep.tile([P, N], U8, name="w_plane", align_bytes=64)
+        nc.vector.quantize_mx(out=w_codes[:].bitcast(FP8X4), scales=w_plane[:], in_=w_grouped[:].rearrange("p t m j -> p (t m j)"))
+
+        x_codes = keep.tile([P, S], U32, name="x_codes", align_bytes=64)
+        for h in range(2):
+            nc.vector.tensor_copy(x_codes[:, h * HALF : (h + 1) * HALF], word_table[:].bitcast(U32).indirect(offsets[:, h * HALF // 16 : (h + 1) * HALF // 16]))
+        pieces = [(0, 0, HALF), (1, 0, HALF), (0, HALF, S), (1, HALF, S), (2, 0, S), (3, 0, S)]
+        banks = {}
+        for t, lo, hi in pieces:
+            banks[t, lo] = psum.tile([P, hi - lo], F32, name=f"bank{t}_{lo}")
+            nc.tensor.matmul_mx(
+                out=banks[t, lo][:],
+                lhsT=w_codes[:, t * P : (t + 1) * P].bitcast(FP8X4),
+                lhsT_scale=w_plane[:, t * P : (t + 1) * P],
+                rhs=x_codes[:, lo:hi].bitcast(FP8X4),
+                rhs_scale=x_plane[:, lo:hi],
+                start=True,
+                stop=True,
+            )
+
+        logits = [keep.tile([P, S], F32, name=f"logits{t}", align_bytes=64) for t in range(PACK)]
+        expd = [keep.tile([P, S], F32, name=f"expd{t}", align_bytes=64) for t in range(PACK)]
+        neg_max = [keep.tile([P, 1], F32, name=f"neg_max{t}") for t in range(PACK)]
+        total = [keep.tile([P, 1], F32, name=f"total{t}") for t in range(PACK)]
+        inv = [keep.tile([P, 1], F32, name=f"inv{t}") for t in range(PACK)]
+        probs = keep.tile([P, PACK, S], F32, name="probs", align_bytes=64)
+        out_rows = out_0.rearrange("(p t) c -> p t c", t=PACK)
+
+        def add(t, lo, hi):
+            nc.vector.tensor_tensor(logits[t][:, lo:hi], banks[t, lo][:], prior_sb[:, lo:hi], ALU.add)
+
+        def top(t):
+            nc.vector.tensor_reduce(neg_max[t][:], logits[t][:], AX.X, ALU.max, negate=True)
+            nc.scalar.activation(expd[t][:], logits[t][:], ACT.Exp, bias=neg_max[t][:], accum_out=total[t][:])
+
+        def norm(t, on_scalar):
+            nc.vector.reciprocal(inv[t][:], total[t][:])
+            if on_scalar:
+                nc.scalar.activation(probs[:, t, :], expd[t][:], ACT.Copy, scale=inv[t][:])
+            else:
+                nc.vector.tensor_scalar(probs[:, t, :], expd[t][:], inv[t][:], None, ALU.mult)
+            nc.sync.dma_start(out=out_rows[:, t, :], in_=probs[:, t, :])
+
+        add(0, 0, HALF)
+        add(1, 0, HALF)
+        add(0, HALF, S)
+        add(1, HALF, S)
+        top(0)
+        add(2, 0, S)
+        top(1)
+        add(3, 0, S)
+        norm(0, True)
+        top(2)
+        norm(1, True)
+        top(3)
+        norm(2, False)
+        norm(3, False)
+
+        y_grouped = keep.tile([P, S, PACK], BF16, name="y_grouped", align_bytes=64)
+        y_dst = y_grouped[:].rearrange("p (c i) t -> p c t i", i=4)
+        y_src = probs[:].rearrange("p t (c i) -> p c t i", i=4)
+        y_codes = keep.tile([P, S], U32, name="y_codes", align_bytes=64)
+        y_plane = keep.tile([P, S], U8, name="y_plane", align_bytes=64)
+        nc.scalar.copy(out=y_dst[:, C_SPLIT // 4 :], in_=y_src[:, C_SPLIT // 4 :])
+        nc.vector.tensor_copy(out=y_dst[:, : HALF // 4], in_=y_src[:, : HALF // 4])
+        nc.vector.tensor_copy(out=y_dst[:, HALF // 4 : C_SPLIT // 4], in_=y_src[:, HALF // 4 : C_SPLIT // 4])
+        words_out = out_1[0].rearrange("p n t -> p (n t)").bitcast(I32)
+        for h in range(2):
+            cols = slice(h * HALF, (h + 1) * HALF)
+            nc.vector.quantize_mx(out=y_codes[:, cols].bitcast(FP8X4), scales=y_plane[:, cols], in_=y_grouped[:, cols, :].rearrange("p c t -> p (c t)"))
+            nc.sync.dma_start(out=words_out[:, cols], in_=y_codes[:, cols].bitcast(I32))
+        for q in range(4):
+            eng = nc.scalar if q % 2 else nc.sync
+            eng.dma_start(out=out_2[0].bitcast(I32)[4 * q : 4 * q + 4, :], in_=y_plane[:].bitcast(I32)[32 * q : 32 * q + 4, :])

@@ -20,7 +20,7 @@ P = 128
 PACK = 4
 HALF = S // 2
 W_SPLIT = 80
-C_SPLIT = 384
+C_SPLIT = 320
 
 
 def tile_picked_phrank_none_po_kernel(tc, x_words, x_scales, w1, prior, offs, out_0, out_1, out_2):
@@ -30,45 +30,64 @@ def tile_picked_phrank_none_po_kernel(tc, x_words, x_scales, w1, prior, offs, ou
         psum = ctx.enter_context(tc.psum_pool(name="psum", bufs=1))
 
         offsets = keep.tile([P, S // 16], U16, name="offsets")
-        scale_table = keep.tile([P, T], U8, name="scale_table", align_bytes=64)
+        scale_table = keep.tile([P, T], U8, name="scale_table", tag="table_then_prior", align_bytes=64)
         word_table = keep.tile([P, T], I32, name="word_table", align_bytes=64)
-        w_raw = keep.tile([P, PACK, N], F32, name="w_raw", align_bytes=64)
-        prior_sb = keep.tile([P, S], F32, name="prior_sb", align_bytes=64)
+        w_raw = [keep.tile([P, 2, N], F32, name=f"w_raw{g}", align_bytes=64) for g in range(2)]
         warm = keep.tile([P, 8], F32, name="warm")
         warm_out = keep.tile([P, 8], F32, name="warm_out")
 
-        nc.sync.dma_start(offsets[:], offs)
-        nc.sync.dma_start(out=w_raw[:], in_=w1.rearrange("(p j) m -> p j m", j=PACK))
-        nc.sync.dma_start(out=word_table[:], in_=x_words[0].rearrange("p n t -> p (n t)").bitcast(I32))
-        nc.sync.dma_start(out=prior_sb[:], in_=prior)
-
+        w_rows = w1.rearrange("(p j) m -> p j m", j=PACK)
         nc.vector.memset(scale_table[:].bitcast(I32), 0)
         nc.vector.memset(warm[:], 0.0)
-        scale_rows = x_scales[0].bitcast(I32).rearrange("(r i) n -> i r n", i=2)
-        for i in range(2):
-            nc.scalar.dma_start(out=scale_table[:].bitcast(I32)[i:P:16, :], in_=scale_rows[i])
+        x_plane = keep.tile([P, S], U8, name="x_plane", align_bytes=64)
+        nc.vector.memset(x_plane[:].bitcast(I32), 0)
         nc.scalar.activation(warm_out[:], warm[:], ACT.Exp)
+        table_rows = x_words[0].rearrange("p n t -> p (n t)").bitcast(I32)
+        nc.sync.dma_start(out=word_table[:, :512], in_=table_rows[:, :512])
+        nc.sync.dma_start(offsets[:], offs)
+        nc.sync.dma_start(out=scale_table[:].bitcast(I32)[0:P:8, :], in_=x_scales[0].bitcast(I32))
+        nc.sync.dma_start(out=word_table[:, 512:], in_=table_rows[:, 512:])
+        for g in range(2):
+            nc.sync.dma_start(out=w_raw[g][:], in_=w_rows[:, 2 * g : 2 * g + 2])
 
         picked_scales = keep.tile([P, S], U8, name="picked_scales", align_bytes=64)
         nc.vector.tensor_copy(picked_scales[:], scale_table[:].indirect(offsets[:]))
-        x_plane = keep.tile([P, S], U8, name="x_plane", align_bytes=64)
-        nc.vector.tensor_copy(x_plane[:].bitcast(I32), picked_scales[:].bitcast(I32))
-        for i in range(2):
-            nc.scalar.dma_start(out=x_plane[:].bitcast(I32)[2 + i : P : 32, :], in_=picked_scales[:].bitcast(I32)[16 + i : P : 32, :])
-
-        w_grouped = keep.tile([P, PACK, P, PACK], BF16, name="w_grouped", align_bytes=64)
-        w_dst = w_grouped[:].rearrange("p t m j -> p m t j")
-        w_src = w_raw[:].rearrange("p j (m t) -> p m t j", t=PACK)
-        nc.vector.tensor_copy(out=w_dst[:, :W_SPLIT], in_=w_src[:, :W_SPLIT])
-        nc.scalar.copy(out=w_dst[:, W_SPLIT:], in_=w_src[:, W_SPLIT:])
-        w_codes = keep.tile([P, N], U32, name="w_codes", align_bytes=64)
-        w_plane = keep.tile([P, N], U8, name="w_plane", align_bytes=64)
-        nc.vector.quantize_mx(out=w_codes[:].bitcast(FP8X4), scales=w_plane[:], in_=w_grouped[:].rearrange("p t m j -> p (t m j)"))
+        for j in range(4):
+            nc.sync.dma_start(out=x_plane[:].bitcast(I32)[j:P:32, :], in_=picked_scales[:].bitcast(I32)[8 * j : P : 32, :])
+        prior_sb = keep.tile([P, S], F32, name="prior_sb", tag="table_then_prior", align_bytes=64)
+        nc.sync.dma_start(out=prior_sb[:], in_=prior)
 
         x_codes = keep.tile([P, S], U32, name="x_codes", align_bytes=64)
-        for h in range(2):
-            nc.vector.tensor_copy(x_codes[:, h * HALF : (h + 1) * HALF], word_table[:].bitcast(U32).indirect(offsets[:, h * HALF // 16 : (h + 1) * HALF // 16]))
-        pieces = [(0, 0, HALF), (1, 0, HALF), (0, HALF, S), (1, HALF, S), (2, 0, S), (3, 0, S)]
+        nc.vector.tensor_copy(x_codes[:], word_table[:].bitcast(U32).indirect(offsets[:]))
+
+        w_codes = keep.tile([P, N], U32, name="w_codes", align_bytes=64)
+        w_plane = keep.tile([P, N], U8, name="w_plane", align_bytes=64)
+        w_grouped = [keep.tile([P, 2, P, PACK], BF16, name=f"w_grouped{u}", align_bytes=64) for u in range(2)]
+
+        def wcast(eng, g, u, e0, e1):
+            src = w_raw[g][:].rearrange("p j (m u e) -> p u m j e", u=2, e=2)[:, u]
+            dst = w_grouped[u][:].rearrange("p e m (g j) -> p g m j e", g=2)[:, g]
+            src = src[:, :, :, e0:e1]
+            dst = dst[:, :, :, e0:e1]
+            if eng == "s":
+                nc.scalar.copy(out=dst, in_=src)
+            else:
+                nc.vector.tensor_copy(out=dst, in_=src)
+
+        def wquant(u, e0, e1):
+            cols = slice((2 * u + e0) * P, (2 * u + e1) * P)
+            nc.vector.quantize_mx(out=w_codes[:, cols].bitcast(FP8X4), scales=w_plane[:, cols], in_=w_grouped[u][:, e0:e1].rearrange("p e m j -> p (e m j)"))
+
+        wcast("v", 0, 0, 0, 2)
+        wcast("s", 0, 1, 0, 2)
+        wcast("v", 1, 0, 0, 1)
+        wcast("v", 1, 0, 1, 2)
+        wcast("s", 1, 1, 0, 2)
+        wquant(0, 0, 1)
+        wquant(0, 1, 2)
+        wquant(1, 0, 2)
+
+        pieces = [(0, 0, HALF), (1, 0, HALF), (1, HALF, S), (0, HALF, S), (2, 0, S), (3, 0, S)]
         banks = {}
         for t, lo, hi in pieces:
             banks[t, lo] = psum.tile([P, hi - lo], F32, name=f"bank{t}_{lo}")
@@ -83,6 +102,7 @@ def tile_picked_phrank_none_po_kernel(tc, x_words, x_scales, w1, prior, offs, ou
             )
 
         logits = [keep.tile([P, S], F32, name=f"logits{t}", align_bytes=64) for t in range(PACK)]
+        scores = [keep.tile([P, S], F32, name=f"scores{t}", align_bytes=64) for t in range(PACK)]
         expd = [keep.tile([P, S], F32, name=f"expd{t}", align_bytes=64) for t in range(PACK)]
         neg_max = [keep.tile([P, 1], F32, name=f"neg_max{t}") for t in range(PACK)]
         total = [keep.tile([P, 1], F32, name=f"total{t}") for t in range(PACK)]
@@ -93,46 +113,96 @@ def tile_picked_phrank_none_po_kernel(tc, x_words, x_scales, w1, prior, offs, ou
         def add(t, lo, hi):
             nc.vector.tensor_tensor(logits[t][:, lo:hi], banks[t, lo][:], prior_sb[:, lo:hi], ALU.add)
 
+        def gadd(t, lo, hi):
+            nc.scalar.copy(scores[t][:, lo:hi], banks[t, lo][:])
+            nc.gpsimd.tensor_tensor(logits[t][:, lo:hi], scores[t][:, lo:hi], prior_sb[:, lo:hi], ALU.add)
+
         def top(t):
             nc.vector.tensor_reduce(neg_max[t][:], logits[t][:], AX.X, ALU.max, negate=True)
+
+        def ex(t):
             nc.scalar.activation(expd[t][:], logits[t][:], ACT.Exp, bias=neg_max[t][:], accum_out=total[t][:])
 
-        def norm(t, on_scalar):
+        def rec(t):
             nc.vector.reciprocal(inv[t][:], total[t][:])
-            if on_scalar:
-                nc.scalar.activation(probs[:, t, :], expd[t][:], ACT.Copy, scale=inv[t][:])
-            else:
-                nc.vector.tensor_scalar(probs[:, t, :], expd[t][:], inv[t][:], None, ALU.mult)
-            nc.sync.dma_start(out=out_rows[:, t, :], in_=probs[:, t, :])
 
-        add(0, 0, HALF)
-        add(1, 0, HALF)
-        add(0, HALF, S)
-        add(1, HALF, S)
-        top(0)
-        add(2, 0, S)
-        top(1)
-        add(3, 0, S)
-        norm(0, True)
-        top(2)
-        norm(1, True)
-        top(3)
-        norm(2, False)
-        norm(3, False)
+        def norm(t, eng, lo=0, hi=S):
+            if eng == "s":
+                nc.scalar.activation(probs[:, t, lo:hi], expd[t][:, lo:hi], ACT.Copy, scale=inv[t][:])
+            elif eng == "g":
+                nc.gpsimd.tensor_scalar(probs[:, t, lo:hi], expd[t][:, lo:hi], inv[t][:], 0.0, ALU.mult, ALU.add)
+            else:
+                nc.vector.tensor_scalar(probs[:, t, lo:hi], expd[t][:, lo:hi], inv[t][:], None, ALU.mult)
+
+        def store(t, eng=nc.sync):
+            eng.dma_start(out=out_rows[:, t, :], in_=probs[:, t, :])
+
 
         y_grouped = keep.tile([P, S, PACK], BF16, name="y_grouped", align_bytes=64)
         y_dst = y_grouped[:].rearrange("p (c i) t -> p c t i", i=4)
         y_src = probs[:].rearrange("p t (c i) -> p c t i", i=4)
         y_codes = keep.tile([P, S], U32, name="y_codes", align_bytes=64)
         y_plane = keep.tile([P, S], U8, name="y_plane", align_bytes=64)
-        nc.scalar.copy(out=y_dst[:, C_SPLIT // 4 :], in_=y_src[:, C_SPLIT // 4 :])
-        nc.vector.tensor_copy(out=y_dst[:, : HALF // 4], in_=y_src[:, : HALF // 4])
-        nc.vector.tensor_copy(out=y_dst[:, HALF // 4 : C_SPLIT // 4], in_=y_src[:, HALF // 4 : C_SPLIT // 4])
         words_out = out_1[0].rearrange("p n t -> p (n t)").bitcast(I32)
-        for h in range(2):
-            cols = slice(h * HALF, (h + 1) * HALF)
-            nc.vector.quantize_mx(out=y_codes[:, cols].bitcast(FP8X4), scales=y_plane[:, cols], in_=y_grouped[:, cols, :].rearrange("p c t -> p (c t)"))
-            nc.sync.dma_start(out=words_out[:, cols], in_=y_codes[:, cols].bitcast(I32))
-        for q in range(4):
-            eng = nc.scalar if q % 2 else nc.sync
+
+        def cast(eng, lo, hi):
+            if eng == "s":
+                nc.scalar.copy(out=y_dst[:, lo // 4 : hi // 4], in_=y_src[:, lo // 4 : hi // 4])
+            else:
+                nc.vector.tensor_copy(out=y_dst[:, lo // 4 : hi // 4], in_=y_src[:, lo // 4 : hi // 4])
+
+        def pcast(eng, u, lo, hi):
+            dst = y_grouped[:].rearrange("p (c i) (u e) -> p u c e i", i=4, u=2)[:, u, lo // 4 : hi // 4]
+            src = probs[:].rearrange("p (u e) (c i) -> p u c e i", i=4, u=2)[:, u, lo // 4 : hi // 4]
+            if eng == "s":
+                nc.scalar.copy(out=dst, in_=src)
+            else:
+                nc.vector.tensor_copy(out=dst, in_=src)
+
+        def quant(lo, hi):
+            nc.vector.quantize_mx(out=y_codes[:, lo:hi].bitcast(FP8X4), scales=y_plane[:, lo:hi], in_=y_grouped[:, lo:hi, :].rearrange("p c t -> p (c t)"))
+
+        def wstore(lo, hi, eng=nc.sync):
+            eng.dma_start(out=words_out[:, lo:hi], in_=y_codes[:, lo:hi].bitcast(I32))
+
+        def sstore(q, eng):
             eng.dma_start(out=out_2[0].bitcast(I32)[4 * q : 4 * q + 4, :], in_=y_plane[:].bitcast(I32)[32 * q : 32 * q + 4, :])
+
+        gadd(0, 0, HALF)
+        add(1, 0, HALF)
+        add(1, HALF, S)
+        gadd(0, HALF, S)
+        top(1)
+        ex(1)
+        add(2, 0, S)
+        top(0)
+        ex(0)
+        rec(1)
+        norm(1, "g")
+        store(1)
+        add(3, 0, S)
+        rec(0)
+        norm(0, "g")
+        store(0)
+        top(2)
+        ex(2)
+        top(3)
+        ex(3)
+        rec(2)
+        norm(2, "v")
+        store(2)
+        rec(3)
+        norm(3, "s", C_SPLIT, S)
+        norm(3, "v", 0, C_SPLIT)
+        store(3)
+        cast("s", C_SPLIT, S)
+        cast("v", 0, HALF)
+        cast("v", HALF, C_SPLIT)
+        quant(0, HALF)
+        wstore(0, HALF)
+        quant(HALF, S)
+        wstore(HALF, S)
+        sstore(0, nc.scalar)
+        sstore(1, nc.scalar)
+        sstore(2, nc.sync)
+        sstore(3, nc.sync)

@@ -18,9 +18,11 @@ AX = mybir.AxisListType
 
 P = 128
 PACK = 4
+QUAD = 32
+BLOCK_PARTS = 8
 HALF = S // 2
-W_SPLIT = 80
-C_SPLIT = 320
+TABLE_LEAD = 512
+VECTOR_COLS = 320
 
 
 def tile_picked_phrank_none_po_kernel(tc, x_words, x_scales, w1, prior, offs, out_0, out_1, out_2):
@@ -33,27 +35,24 @@ def tile_picked_phrank_none_po_kernel(tc, x_words, x_scales, w1, prior, offs, ou
         scale_table = keep.tile([P, T], U8, name="scale_table", tag="table_then_prior", align_bytes=64)
         word_table = keep.tile([P, T], I32, name="word_table", align_bytes=64)
         w_raw = [keep.tile([P, 2, N], F32, name=f"w_raw{g}", align_bytes=64) for g in range(2)]
-        warm = keep.tile([P, 8], F32, name="warm")
-        warm_out = keep.tile([P, 8], F32, name="warm_out")
 
-        w_rows = w1.rearrange("(p j) m -> p j m", j=PACK)
         nc.vector.memset(scale_table[:].bitcast(I32), 0)
-        nc.vector.memset(warm[:], 0.0)
         x_plane = keep.tile([P, S], U8, name="x_plane", align_bytes=64)
         nc.vector.memset(x_plane[:].bitcast(I32), 0)
-        nc.scalar.activation(warm_out[:], warm[:], ACT.Exp)
+
+        w_rows = w1.rearrange("(p j) m -> p j m", j=PACK)
         table_rows = x_words[0].rearrange("p n t -> p (n t)").bitcast(I32)
-        nc.sync.dma_start(out=word_table[:, :512], in_=table_rows[:, :512])
+        nc.sync.dma_start(out=word_table[:, :TABLE_LEAD], in_=table_rows[:, :TABLE_LEAD])
         nc.sync.dma_start(offsets[:], offs)
-        nc.sync.dma_start(out=scale_table[:].bitcast(I32)[0:P:8, :], in_=x_scales[0].bitcast(I32))
-        nc.sync.dma_start(out=word_table[:, 512:], in_=table_rows[:, 512:])
+        nc.sync.dma_start(out=scale_table[:].bitcast(I32)[0:P:BLOCK_PARTS, :], in_=x_scales[0].bitcast(I32))
+        nc.sync.dma_start(out=word_table[:, TABLE_LEAD:], in_=table_rows[:, TABLE_LEAD:])
         for g in range(2):
             nc.sync.dma_start(out=w_raw[g][:], in_=w_rows[:, 2 * g : 2 * g + 2])
 
         picked_scales = keep.tile([P, S], U8, name="picked_scales", align_bytes=64)
         nc.vector.tensor_copy(picked_scales[:], scale_table[:].indirect(offsets[:]))
-        for j in range(4):
-            nc.sync.dma_start(out=x_plane[:].bitcast(I32)[j:P:32, :], in_=picked_scales[:].bitcast(I32)[8 * j : P : 32, :])
+        for r in range(4):
+            nc.sync.dma_start(out=x_plane[:].bitcast(I32)[r:P:QUAD, :], in_=picked_scales[:].bitcast(I32)[BLOCK_PARTS * r : P : QUAD, :])
         prior_sb = keep.tile([P, S], F32, name="prior_sb", tag="table_then_prior", align_bytes=64)
         nc.sync.dma_start(out=prior_sb[:], in_=prior)
 
@@ -64,45 +63,27 @@ def tile_picked_phrank_none_po_kernel(tc, x_words, x_scales, w1, prior, offs, ou
         w_plane = keep.tile([P, N], U8, name="w_plane", align_bytes=64)
         w_grouped = [keep.tile([P, 2, P, PACK], BF16, name=f"w_grouped{u}", align_bytes=64) for u in range(2)]
 
-        def wcast(eng, g, u, e0, e1):
-            src = w_raw[g][:].rearrange("p j (m u e) -> p u m j e", u=2, e=2)[:, u]
-            dst = w_grouped[u][:].rearrange("p e m (g j) -> p g m j e", g=2)[:, g]
-            src = src[:, :, :, e0:e1]
-            dst = dst[:, :, :, e0:e1]
-            if eng == "s":
-                nc.scalar.copy(out=dst, in_=src)
-            else:
-                nc.vector.tensor_copy(out=dst, in_=src)
+        def w_views(g, u):
+            dst = w_grouped[u][:].rearrange("p e m (g i) -> p g m i e", g=2)[:, g]
+            src = w_raw[g][:].rearrange("p i (m u e) -> p u m i e", u=2, e=2)[:, u]
+            return dst, src
 
-        def wquant(u, e0, e1):
+        def w_quantise(u, e0, e1):
             cols = slice((2 * u + e0) * P, (2 * u + e1) * P)
             nc.vector.quantize_mx(out=w_codes[:, cols].bitcast(FP8X4), scales=w_plane[:, cols], in_=w_grouped[u][:, e0:e1].rearrange("p e m j -> p (e m j)"))
 
-        wcast("v", 0, 0, 0, 2)
-        wcast("s", 0, 1, 0, 2)
-        wcast("v", 1, 0, 0, 1)
-        wcast("v", 1, 0, 1, 2)
-        wcast("s", 1, 1, 0, 2)
-        wquant(0, 0, 1)
-        wquant(0, 1, 2)
-        wquant(1, 0, 2)
-
-        pieces = [(0, 0, HALF), (1, 0, HALF), (1, HALF, S), (0, HALF, S), (2, 0, S), (3, 0, S)]
-        banks = {}
-        for t, lo, hi in pieces:
-            banks[t, lo] = psum.tile([P, hi - lo], F32, name=f"bank{t}_{lo}")
-            nc.tensor.matmul_mx(
-                out=banks[t, lo][:],
-                lhsT=w_codes[:, t * P : (t + 1) * P].bitcast(FP8X4),
-                lhsT_scale=w_plane[:, t * P : (t + 1) * P],
-                rhs=x_codes[:, lo:hi].bitcast(FP8X4),
-                rhs_scale=x_plane[:, lo:hi],
-                start=True,
-                stop=True,
-            )
+        nc.vector.tensor_copy(*w_views(0, 0))
+        nc.scalar.activation(*w_views(0, 1), ACT.Copy)
+        last_dst, last_src = w_views(1, 0)
+        for e in range(2):
+            nc.vector.tensor_copy(last_dst[:, :, :, e : e + 1], last_src[:, :, :, e : e + 1])
+        nc.scalar.activation(*w_views(1, 1), ACT.Copy)
+        w_quantise(0, 0, 1)
+        w_quantise(0, 1, 2)
+        w_quantise(1, 0, 2)
 
         logits = [keep.tile([P, S], F32, name=f"logits{t}", align_bytes=64) for t in range(PACK)]
-        scores = [keep.tile([P, S], F32, name=f"scores{t}", align_bytes=64) for t in range(PACK)]
+        staged = keep.tile([P, S], F32, name="staged", align_bytes=64)
         expd = [keep.tile([P, S], F32, name=f"expd{t}", align_bytes=64) for t in range(PACK)]
         neg_max = [keep.tile([P, 1], F32, name=f"neg_max{t}") for t in range(PACK)]
         total = [keep.tile([P, 1], F32, name=f"total{t}") for t in range(PACK)]
@@ -110,99 +91,79 @@ def tile_picked_phrank_none_po_kernel(tc, x_words, x_scales, w1, prior, offs, ou
         probs = keep.tile([P, PACK, S], F32, name="probs", align_bytes=64)
         out_rows = out_0.rearrange("(p t) c -> p t c", t=PACK)
 
-        def add(t, lo, hi):
-            nc.vector.tensor_tensor(logits[t][:, lo:hi], banks[t, lo][:], prior_sb[:, lo:hi], ALU.add)
+        def scores(t, cols, ring):
+            bank = psum.tile([P, cols.stop - cols.start], F32, name=f"bank{t}_{cols.start}", tag=ring, bufs=2)
+            nc.tensor.matmul_mx(
+                out=bank[:],
+                lhsT=w_codes[:, t * P : (t + 1) * P].bitcast(FP8X4),
+                lhsT_scale=w_plane[:, t * P : (t + 1) * P],
+                rhs=x_codes[:, cols].bitcast(FP8X4),
+                rhs_scale=x_plane[:, cols],
+                start=True,
+                stop=True,
+            )
+            return bank
 
-        def gadd(t, lo, hi):
-            nc.scalar.copy(scores[t][:, lo:hi], banks[t, lo][:])
-            nc.gpsimd.tensor_tensor(logits[t][:, lo:hi], scores[t][:, lo:hi], prior_sb[:, lo:hi], ALU.add)
+        def add_prior(t, cols, bank):
+            nc.vector.tensor_tensor(logits[t][:, cols], bank[:], prior_sb[:, cols], ALU.add)
 
-        def top(t):
+        def add_prior_off_vector(t, cols, bank):
+            nc.scalar.copy(staged[:, cols], bank[:])
+            nc.gpsimd.tensor_tensor(logits[t][:, cols], staged[:, cols], prior_sb[:, cols], ALU.add)
+
+        def exponentiate(t):
             nc.vector.tensor_reduce(neg_max[t][:], logits[t][:], AX.X, ALU.max, negate=True)
-
-        def ex(t):
             nc.scalar.activation(expd[t][:], logits[t][:], ACT.Exp, bias=neg_max[t][:], accum_out=total[t][:])
 
-        def rec(t):
+        def scale_on_scalar(t, cols):
+            nc.scalar.activation(probs[:, t, cols], expd[t][:, cols], ACT.Copy, scale=inv[t][:])
+
+        def scale_on_vector(t, cols):
+            nc.vector.tensor_scalar(probs[:, t, cols], expd[t][:, cols], inv[t][:], None, ALU.mult)
+
+        def store_rows(t):
+            nc.sync.dma_start(out=out_rows[:, t, :], in_=probs[:, t, :])
+
+        halves = [slice(0, HALF), slice(HALF, S)]
+        whole = slice(0, S)
+
+        banks0 = [scores(0, cols, "for_vector") for cols in halves]
+        banks1 = [scores(1, cols, "for_scalar") for cols in halves]
+        for cols, bank in zip(halves, banks0):
+            add_prior(0, cols, bank)
+        bank2 = scores(2, whole, "for_vector")
+        bank3 = scores(3, whole, "for_vector")
+        for cols, bank in zip(halves, banks1):
+            add_prior_off_vector(1, cols, bank)
+        exponentiate(0)
+        add_prior(2, whole, bank2)
+        add_prior(3, whole, bank3)
+        nc.vector.reciprocal(inv[0][:], total[0][:])
+        scale_on_scalar(0, whole)
+        store_rows(0)
+        for t in (2, 1, 3):
+            exponentiate(t)
+        for t in (2, 1):
             nc.vector.reciprocal(inv[t][:], total[t][:])
-
-        def norm(t, eng, lo=0, hi=S):
-            if eng == "s":
-                nc.scalar.activation(probs[:, t, lo:hi], expd[t][:, lo:hi], ACT.Copy, scale=inv[t][:])
-            elif eng == "g":
-                nc.gpsimd.tensor_scalar(probs[:, t, lo:hi], expd[t][:, lo:hi], inv[t][:], 0.0, ALU.mult, ALU.add)
-            else:
-                nc.vector.tensor_scalar(probs[:, t, lo:hi], expd[t][:, lo:hi], inv[t][:], None, ALU.mult)
-
-        def store(t, eng=nc.sync):
-            eng.dma_start(out=out_rows[:, t, :], in_=probs[:, t, :])
-
+            scale_on_vector(t, whole)
+            store_rows(t)
+        nc.vector.reciprocal(inv[3][:], total[3][:])
+        scale_on_scalar(3, slice(VECTOR_COLS, S))
+        scale_on_vector(3, slice(0, VECTOR_COLS))
+        store_rows(3)
 
         y_grouped = keep.tile([P, S, PACK], BF16, name="y_grouped", align_bytes=64)
         y_dst = y_grouped[:].rearrange("p (c i) t -> p c t i", i=4)
         y_src = probs[:].rearrange("p t (c i) -> p c t i", i=4)
         y_codes = keep.tile([P, S], U32, name="y_codes", align_bytes=64)
         y_plane = keep.tile([P, S], U8, name="y_plane", align_bytes=64)
+        nc.scalar.copy(out=y_dst[:, VECTOR_COLS // 4 :], in_=y_src[:, VECTOR_COLS // 4 :])
+        for lo, hi in ((0, HALF), (HALF, VECTOR_COLS)):
+            nc.vector.tensor_copy(out=y_dst[:, lo // 4 : hi // 4], in_=y_src[:, lo // 4 : hi // 4])
         words_out = out_1[0].rearrange("p n t -> p (n t)").bitcast(I32)
-
-        def cast(eng, lo, hi):
-            if eng == "s":
-                nc.scalar.copy(out=y_dst[:, lo // 4 : hi // 4], in_=y_src[:, lo // 4 : hi // 4])
-            else:
-                nc.vector.tensor_copy(out=y_dst[:, lo // 4 : hi // 4], in_=y_src[:, lo // 4 : hi // 4])
-
-        def pcast(eng, u, lo, hi):
-            dst = y_grouped[:].rearrange("p (c i) (u e) -> p u c e i", i=4, u=2)[:, u, lo // 4 : hi // 4]
-            src = probs[:].rearrange("p (u e) (c i) -> p u c e i", i=4, u=2)[:, u, lo // 4 : hi // 4]
-            if eng == "s":
-                nc.scalar.copy(out=dst, in_=src)
-            else:
-                nc.vector.tensor_copy(out=dst, in_=src)
-
-        def quant(lo, hi):
-            nc.vector.quantize_mx(out=y_codes[:, lo:hi].bitcast(FP8X4), scales=y_plane[:, lo:hi], in_=y_grouped[:, lo:hi, :].rearrange("p c t -> p (c t)"))
-
-        def wstore(lo, hi, eng=nc.sync):
-            eng.dma_start(out=words_out[:, lo:hi], in_=y_codes[:, lo:hi].bitcast(I32))
-
-        def sstore(q, eng):
-            eng.dma_start(out=out_2[0].bitcast(I32)[4 * q : 4 * q + 4, :], in_=y_plane[:].bitcast(I32)[32 * q : 32 * q + 4, :])
-
-        gadd(0, 0, HALF)
-        add(1, 0, HALF)
-        add(1, HALF, S)
-        gadd(0, HALF, S)
-        top(1)
-        ex(1)
-        add(2, 0, S)
-        top(0)
-        ex(0)
-        rec(1)
-        norm(1, "g")
-        store(1)
-        add(3, 0, S)
-        rec(0)
-        norm(0, "g")
-        store(0)
-        top(2)
-        ex(2)
-        top(3)
-        ex(3)
-        rec(2)
-        norm(2, "v")
-        store(2)
-        rec(3)
-        norm(3, "s", C_SPLIT, S)
-        norm(3, "v", 0, C_SPLIT)
-        store(3)
-        cast("s", C_SPLIT, S)
-        cast("v", 0, HALF)
-        cast("v", HALF, C_SPLIT)
-        quant(0, HALF)
-        wstore(0, HALF)
-        quant(HALF, S)
-        wstore(HALF, S)
-        sstore(0, nc.scalar)
-        sstore(1, nc.scalar)
-        sstore(2, nc.sync)
-        sstore(3, nc.sync)
+        for cols in halves:
+            nc.vector.quantize_mx(out=y_codes[:, cols].bitcast(FP8X4), scales=y_plane[:, cols], in_=y_grouped[:, cols, :].rearrange("p c t -> p (c t)"))
+            nc.sync.dma_start(out=words_out[:, cols], in_=y_codes[:, cols].bitcast(I32))
+        for q in range(4):
+            queue = nc.scalar if q < 2 else nc.sync
+            queue.dma_start(out=out_2[0].bitcast(I32)[4 * q : 4 * q + 4, :], in_=y_plane[:].bitcast(I32)[QUAD * q : QUAD * q + 4, :])

@@ -21,7 +21,7 @@ PACK = 4
 QUAD = 32
 BLOCK_PARTS = 8
 HALF = S // 2
-TABLE_LEAD = 512
+TABLE_LEAD = 768
 VECTOR_COLS = 320
 
 

@@ -21,7 +21,6 @@ PACK = 4
 QUAD = 32
 BLOCK_PARTS = 8
 HALF = S // 2
-TABLE_LEAD = 768
 VECTOR_COLS = 320
 
 
@@ -34,7 +33,7 @@ def tile_picked_phrank_none_po_kernel(tc, x_words, x_scales, w1, prior, offs, ou
         offsets = keep.tile([P, S // 16], U16, name="offsets")
         scale_table = keep.tile([P, T], U8, name="scale_table", tag="table_then_prior", align_bytes=64)
         word_table = keep.tile([P, T], I32, name="word_table", align_bytes=64)
-        w_raw = [keep.tile([P, 2, N], F32, name=f"w_raw{g}", align_bytes=64) for g in range(2)]
+        w_raw = keep.tile([P, PACK, N], F32, name="w_raw", align_bytes=64)
 
         nc.vector.memset(scale_table[:].bitcast(I32), 0)
         x_plane = keep.tile([P, S], U8, name="x_plane", align_bytes=64)
@@ -42,12 +41,11 @@ def tile_picked_phrank_none_po_kernel(tc, x_words, x_scales, w1, prior, offs, ou
 
         w_rows = w1.rearrange("(p j) m -> p j m", j=PACK)
         table_rows = x_words[0].rearrange("p n t -> p (n t)").bitcast(I32)
-        nc.sync.dma_start(out=word_table[:, :TABLE_LEAD], in_=table_rows[:, :TABLE_LEAD])
+        nc.sync.dma_start(out=w_raw[:, :2], in_=w_rows[:, :2])
         nc.sync.dma_start(offsets[:], offs)
         nc.sync.dma_start(out=scale_table[:].bitcast(I32)[0:P:BLOCK_PARTS, :], in_=x_scales[0].bitcast(I32))
-        nc.sync.dma_start(out=word_table[:, TABLE_LEAD:], in_=table_rows[:, TABLE_LEAD:])
-        for g in range(2):
-            nc.sync.dma_start(out=w_raw[g][:], in_=w_rows[:, 2 * g : 2 * g + 2])
+        nc.sync.dma_start(out=w_raw[:, 2:], in_=w_rows[:, 2:])
+        nc.sync.dma_start(out=word_table[:], in_=table_rows)
 
         picked_scales = keep.tile([P, S], U8, name="picked_scales", align_bytes=64)
         nc.vector.tensor_copy(picked_scales[:], scale_table[:].indirect(offsets[:]))
@@ -56,31 +54,28 @@ def tile_picked_phrank_none_po_kernel(tc, x_words, x_scales, w1, prior, offs, ou
         prior_sb = keep.tile([P, S], F32, name="prior_sb", tag="table_then_prior", align_bytes=64)
         nc.sync.dma_start(out=prior_sb[:], in_=prior)
 
-        x_codes = keep.tile([P, S], U32, name="x_codes", align_bytes=64)
-        nc.vector.tensor_copy(x_codes[:], word_table[:].bitcast(U32).indirect(offsets[:]))
-
         w_codes = keep.tile([P, N], U32, name="w_codes", align_bytes=64)
         w_plane = keep.tile([P, N], U8, name="w_plane", align_bytes=64)
         w_grouped = [keep.tile([P, 2, P, PACK], BF16, name=f"w_grouped{u}", align_bytes=64) for u in range(2)]
 
-        def w_views(g, u):
-            dst = w_grouped[u][:].rearrange("p e m (g i) -> p g m i e", g=2)[:, g]
-            src = w_raw[g][:].rearrange("p i (m u e) -> p u m i e", u=2, e=2)[:, u]
+        def w_views(u):
+            dst = w_grouped[u][:].rearrange("p e m j -> p m j e")
+            src = w_raw[:].rearrange("p j (m u e) -> p u m j e", u=2, e=2)[:, u]
             return dst, src
 
-        def w_quantise(u, e0, e1):
-            cols = slice((2 * u + e0) * P, (2 * u + e1) * P)
-            nc.vector.quantize_mx(out=w_codes[:, cols].bitcast(FP8X4), scales=w_plane[:, cols], in_=w_grouped[u][:, e0:e1].rearrange("p e m j -> p (e m j)"))
+        nc.vector.tensor_copy(*w_views(0))
+        dst, src = w_views(1)
+        for g in range(2):
+            nc.scalar.activation(dst[:, :, 2 * g : 2 * g + 2], src[:, :, 2 * g : 2 * g + 2], ACT.Copy)
+        for u in range(2):
+            cols = slice(2 * u * P, 2 * (u + 1) * P)
+            nc.vector.quantize_mx(out=w_codes[:, cols].bitcast(FP8X4), scales=w_plane[:, cols], in_=w_grouped[u][:].rearrange("p e m j -> p (e m j)"))
 
-        nc.vector.tensor_copy(*w_views(0, 0))
-        nc.scalar.activation(*w_views(0, 1), ACT.Copy)
-        last_dst, last_src = w_views(1, 0)
-        for e in range(2):
-            nc.vector.tensor_copy(last_dst[:, :, :, e : e + 1], last_src[:, :, :, e : e + 1])
-        nc.scalar.activation(*w_views(1, 1), ACT.Copy)
-        w_quantise(0, 0, 1)
-        w_quantise(0, 1, 2)
-        w_quantise(1, 0, 2)
+        halves = [slice(0, HALF), slice(HALF, S)]
+        whole = slice(0, S)
+        x_codes = [keep.tile([P, HALF], U32, name=f"x_codes{h}", align_bytes=64) for h in range(2)]
+        for h in range(2):
+            nc.vector.tensor_copy(x_codes[h][:], word_table[:].bitcast(U32).indirect(offsets[:, h * HALF // 16 : (h + 1) * HALF // 16]))
 
         logits = [keep.tile([P, S], F32, name=f"logits{t}", align_bytes=64) for t in range(PACK)]
         staged = keep.tile([P, S], F32, name="staged", align_bytes=64)
@@ -91,24 +86,26 @@ def tile_picked_phrank_none_po_kernel(tc, x_words, x_scales, w1, prior, offs, ou
         probs = keep.tile([P, PACK, S], F32, name="probs", align_bytes=64)
         out_rows = out_0.rearrange("(p t) c -> p t c", t=PACK)
 
-        def scores(t, cols, ring):
-            bank = psum.tile([P, cols.stop - cols.start], F32, name=f"bank{t}_{cols.start}", tag=ring, bufs=2)
+        def scores(t, h):
+            bank = psum.tile([P, HALF], F32, name=f"bank{t}_{h}")
             nc.tensor.matmul_mx(
                 out=bank[:],
                 lhsT=w_codes[:, t * P : (t + 1) * P].bitcast(FP8X4),
                 lhsT_scale=w_plane[:, t * P : (t + 1) * P],
-                rhs=x_codes[:, cols].bitcast(FP8X4),
-                rhs_scale=x_plane[:, cols],
+                rhs=x_codes[h][:].bitcast(FP8X4),
+                rhs_scale=x_plane[:, halves[h]],
                 start=True,
                 stop=True,
             )
             return bank
 
-        def add_prior(t, cols, bank):
-            nc.vector.tensor_tensor(logits[t][:, cols], bank[:], prior_sb[:, cols], ALU.add)
+        def add_prior(t, h):
+            cols = halves[h]
+            nc.vector.tensor_tensor(logits[t][:, cols], scores(t, h)[:], prior_sb[:, cols], ALU.add)
 
-        def add_prior_off_vector(t, cols, bank):
-            nc.scalar.copy(staged[:, cols], bank[:])
+        def add_prior_off_vector(t, h):
+            cols = halves[h]
+            nc.scalar.copy(staged[:, cols], scores(t, h)[:])
             nc.gpsimd.tensor_tensor(logits[t][:, cols], staged[:, cols], prior_sb[:, cols], ALU.add)
 
         def exponentiate(t):
@@ -124,33 +121,27 @@ def tile_picked_phrank_none_po_kernel(tc, x_words, x_scales, w1, prior, offs, ou
         def store_rows(t):
             nc.sync.dma_start(out=out_rows[:, t, :], in_=probs[:, t, :])
 
-        halves = [slice(0, HALF), slice(HALF, S)]
-        whole = slice(0, S)
-
-        banks0 = [scores(0, cols, "for_vector") for cols in halves]
-        banks1 = [scores(1, cols, "for_scalar") for cols in halves]
-        for cols, bank in zip(halves, banks0):
-            add_prior(0, cols, bank)
-        bank2 = scores(2, whole, "for_vector")
-        bank3 = scores(3, whole, "for_vector")
-        for cols, bank in zip(halves, banks1):
-            add_prior_off_vector(1, cols, bank)
+        for h in range(2):
+            add_prior(0, h)
+            add_prior(2, h)
         exponentiate(0)
-        add_prior(2, whole, bank2)
-        add_prior(3, whole, bank3)
+        for h in range(2):
+            add_prior_off_vector(1, h)
+            add_prior(3, h)
+        exponentiate(2)
         nc.vector.reciprocal(inv[0][:], total[0][:])
-        scale_on_scalar(0, whole)
+        nc.gpsimd.tensor_scalar(probs[:, 0, :], expd[0][:], inv[0][:], 0.0, ALU.mult, ALU.add)
         store_rows(0)
-        for t in (2, 1, 3):
+        for t in (3, 1):
             exponentiate(t)
-        for t in (2, 1):
+        for t in (2, 3):
             nc.vector.reciprocal(inv[t][:], total[t][:])
             scale_on_vector(t, whole)
             store_rows(t)
-        nc.vector.reciprocal(inv[3][:], total[3][:])
-        scale_on_scalar(3, slice(VECTOR_COLS, S))
-        scale_on_vector(3, slice(0, VECTOR_COLS))
-        store_rows(3)
+        nc.vector.reciprocal(inv[1][:], total[1][:])
+        scale_on_scalar(1, slice(VECTOR_COLS, S))
+        scale_on_vector(1, slice(0, VECTOR_COLS))
+        store_rows(1)
 
         y_grouped = keep.tile([P, S, PACK], BF16, name="y_grouped", align_bytes=64)
         y_dst = y_grouped[:].rearrange("p (c i) t -> p c t i", i=4)

@@ -124,18 +124,17 @@ def tile_picked_phrank_none_po_kernel(tc, x_words, x_scales, w1, prior, offs, ou
         for h in range(2):
             add_prior(0, h)
             add_prior(2, h)
-        exponentiate(0)
         for h in range(2):
             add_prior_off_vector(1, h)
+        exponentiate(0)
+        for h in range(2):
             add_prior(3, h)
         exponentiate(2)
-        nc.vector.reciprocal(inv[0][:], total[0][:])
-        nc.gpsimd.tensor_scalar(probs[:, 0, :], expd[0][:], inv[0][:], 0.0, ALU.mult, ALU.add)
-        store_rows(0)
         for t in (3, 1):
             exponentiate(t)
-        for t in (2, 3):
+        for t in (0, 2, 3):
             nc.vector.reciprocal(inv[t][:], total[t][:])
+        for t in (0, 2, 3):
             scale_on_vector(t, whole)
             store_rows(t)
         nc.vector.reciprocal(inv[1][:], total[1][:])

@@ -50,7 +50,7 @@ def tile_picked_phrank_none_po_kernel(tc, x_words, x_scales, w1, prior, offs, ou
         picked_scales = keep.tile([P, S], U8, name="picked_scales", align_bytes=64)
         nc.vector.tensor_copy(picked_scales[:], scale_table[:].indirect(offsets[:]))
         for r in range(4):
-            nc.sync.dma_start(out=x_plane[:].bitcast(I32)[r:P:QUAD, :], in_=picked_scales[:].bitcast(I32)[BLOCK_PARTS * r : P : QUAD, :])
+            nc.scalar.dma_start(out=x_plane[:].bitcast(I32)[r:P:QUAD, :], in_=picked_scales[:].bitcast(I32)[BLOCK_PARTS * r : P : QUAD, :])
         prior_sb = keep.tile([P, S], F32, name="prior_sb", tag="table_then_prior", align_bytes=64)
         nc.sync.dma_start(out=prior_sb[:], in_=prior)
 
@@ -63,10 +63,10 @@ def tile_picked_phrank_none_po_kernel(tc, x_words, x_scales, w1, prior, offs, ou
             src = w_raw[:].rearrange("p j (m u e) -> p u m j e", u=2, e=2)[:, u]
             return dst, src
 
-        nc.vector.tensor_copy(*w_views(0))
         dst, src = w_views(1)
-        for g in range(2):
-            nc.scalar.activation(dst[:, :, 2 * g : 2 * g + 2], src[:, :, 2 * g : 2 * g + 2], ACT.Copy)
+        nc.scalar.activation(dst[:, :, :2], src[:, :, :2], ACT.Copy)
+        nc.vector.tensor_copy(*w_views(0))
+        nc.vector.tensor_copy(dst[:, :, 2:], src[:, :, 2:])
         for u in range(2):
             cols = slice(2 * u * P, 2 * (u + 1) * P)
             nc.vector.quantize_mx(out=w_codes[:, cols].bitcast(FP8X4), scales=w_plane[:, cols], in_=w_grouped[u][:].rearrange("p e m j -> p (e m j)"))

@@ -21,7 +21,8 @@ PACK = 4
 QUAD = 32
 BLOCK_PARTS = 8
 HALF = S // 2
-VECTOR_COLS = 320
+QUARTER = S // 4
+VECTOR_COLS = 352
 
 
 def tile_picked_phrank_none_po_kernel(tc, x_words, x_scales, w1, prior, offs, out_0, out_1, out_2):
@@ -130,16 +131,20 @@ def tile_picked_phrank_none_po_kernel(tc, x_words, x_scales, w1, prior, offs, ou
         for h in range(2):
             add_prior(3, h)
         exponentiate(2)
+        nc.vector.reciprocal(inv[0][:], total[0][:])
+        nc.gpsimd.tensor_scalar(probs[:, 0, :], expd[0][:], inv[0][:], 0.0, ALU.mult, ALU.add)
+        store_rows(0)
         for t in (3, 1):
             exponentiate(t)
-        for t in (0, 2, 3):
+        for t in (2, 3):
             nc.vector.reciprocal(inv[t][:], total[t][:])
-        for t in (0, 2, 3):
+        for t in (2, 3):
             scale_on_vector(t, whole)
             store_rows(t)
         nc.vector.reciprocal(inv[1][:], total[1][:])
         scale_on_scalar(1, slice(VECTOR_COLS, S))
-        scale_on_vector(1, slice(0, VECTOR_COLS))
+        scale_on_vector(1, slice(0, QUARTER))
+        scale_on_vector(1, slice(QUARTER, VECTOR_COLS))
         store_rows(1)
 
         y_grouped = keep.tile([P, S, PACK], BF16, name="y_grouped", align_bytes=64)
@@ -148,11 +153,12 @@ def tile_picked_phrank_none_po_kernel(tc, x_words, x_scales, w1, prior, offs, ou
         y_codes = keep.tile([P, S], U32, name="y_codes", align_bytes=64)
         y_plane = keep.tile([P, S], U8, name="y_plane", align_bytes=64)
         nc.scalar.copy(out=y_dst[:, VECTOR_COLS // 4 :], in_=y_src[:, VECTOR_COLS // 4 :])
-        for lo, hi in ((0, HALF), (HALF, VECTOR_COLS)):
+        for lo, hi in ((0, QUARTER), (QUARTER, HALF), (HALF, VECTOR_COLS)):
             nc.vector.tensor_copy(out=y_dst[:, lo // 4 : hi // 4], in_=y_src[:, lo // 4 : hi // 4])
         words_out = out_1[0].rearrange("p n t -> p (n t)").bitcast(I32)
-        for cols in halves:
+        for cols in (slice(0, QUARTER), slice(QUARTER, HALF), halves[1]):
             nc.vector.quantize_mx(out=y_codes[:, cols].bitcast(FP8X4), scales=y_plane[:, cols], in_=y_grouped[:, cols, :].rearrange("p c t -> p (c t)"))
+        for cols in halves:
             nc.sync.dma_start(out=words_out[:, cols], in_=y_codes[:, cols].bitcast(I32))
         for q in range(4):
             queue = nc.scalar if q < 2 else nc.sync

@@ -22,6 +22,7 @@ QUAD = 32
 BLOCK_PARTS = 8
 HALF = S // 2
 QUARTER = S // 4
+W_LEAD = N + N // 2
 VECTOR_COLS = 352
 
 
@@ -40,12 +41,13 @@ def tile_picked_phrank_none_po_kernel(tc, x_words, x_scales, w1, prior, offs, ou
         x_plane = keep.tile([P, S], U8, name="x_plane", align_bytes=64)
         nc.vector.memset(x_plane[:].bitcast(I32), 0)
 
-        w_rows = w1.rearrange("(p j) m -> p j m", j=PACK)
         table_rows = x_words[0].rearrange("p n t -> p (n t)").bitcast(I32)
-        nc.sync.dma_start(out=w_raw[:, :2], in_=w_rows[:, :2])
+        w_flat = w_raw[:].rearrange("p j m -> p (j m)")
+        w_runs = w1.rearrange("(p j) m -> p (j m)", j=PACK)
+        nc.sync.dma_start(out=w_flat[:, :W_LEAD], in_=w_runs[:, :W_LEAD])
         nc.sync.dma_start(offsets[:], offs)
         nc.sync.dma_start(out=scale_table[:].bitcast(I32)[0:P:BLOCK_PARTS, :], in_=x_scales[0].bitcast(I32))
-        nc.sync.dma_start(out=w_raw[:, 2:], in_=w_rows[:, 2:])
+        nc.sync.dma_start(out=w_flat[:, W_LEAD:], in_=w_runs[:, W_LEAD:])
         nc.sync.dma_start(out=word_table[:], in_=table_rows)
 
         picked_scales = keep.tile([P, S], U8, name="picked_scales", align_bytes=64)
@@ -53,7 +55,8 @@ def tile_picked_phrank_none_po_kernel(tc, x_words, x_scales, w1, prior, offs, ou
         for r in range(4):
             nc.scalar.dma_start(out=x_plane[:].bitcast(I32)[r:P:QUAD, :], in_=picked_scales[:].bitcast(I32)[BLOCK_PARTS * r : P : QUAD, :])
         prior_sb = keep.tile([P, S], F32, name="prior_sb", tag="table_then_prior", align_bytes=64)
-        nc.sync.dma_start(out=prior_sb[:], in_=prior)
+        for lo in (0, HALF):
+            nc.sync.dma_start(out=prior_sb[:, lo : lo + HALF], in_=prior[:, lo : lo + HALF])
 
         w_codes = keep.tile([P, N], U32, name="w_codes", align_bytes=64)
         w_plane = keep.tile([P, N], U8, name="w_plane", align_bytes=64)
@@ -65,9 +68,10 @@ def tile_picked_phrank_none_po_kernel(tc, x_words, x_scales, w1, prior, offs, ou
             return dst, src
 
         dst, src = w_views(1)
-        nc.scalar.activation(dst[:, :, :2], src[:, :, :2], ACT.Copy)
+        nc.scalar.activation(dst[:, : P // 2, :2], src[:, : P // 2, :2], ACT.Copy)
         nc.vector.tensor_copy(*w_views(0))
-        nc.vector.tensor_copy(dst[:, :, 2:], src[:, :, 2:])
+        nc.vector.tensor_copy(dst[:, : P // 2, 2:], src[:, : P // 2, 2:])
+        nc.vector.tensor_copy(dst[:, P // 2 :], src[:, P // 2 :])
         for u in range(2):
             cols = slice(2 * u * P, 2 * (u + 1) * P)
             nc.vector.quantize_mx(out=w_codes[:, cols].bitcast(FP8X4), scales=w_plane[:, cols], in_=w_grouped[u][:].rearrange("p e m j -> p (e m j)"))

@@ -23,6 +23,8 @@ BLOCK_PARTS = 8
 HALF = S // 2
 QUARTER = S // 4
 W_LEAD = N + N // 2
+EARLY_WORDS = 16
+LATE_WORDS = 32
 VECTOR_COLS = 352
 
 
@@ -68,10 +70,11 @@ def tile_picked_phrank_none_po_kernel(tc, x_words, x_scales, w1, prior, offs, ou
             return dst, src
 
         dst, src = w_views(1)
-        nc.scalar.activation(dst[:, : P // 2, :2], src[:, : P // 2, :2], ACT.Copy)
+        nc.scalar.activation(dst[:, :EARLY_WORDS, :2], src[:, :EARLY_WORDS, :2], ACT.Copy)
         nc.vector.tensor_copy(*w_views(0))
-        nc.vector.tensor_copy(dst[:, : P // 2, 2:], src[:, : P // 2, 2:])
-        nc.vector.tensor_copy(dst[:, P // 2 :], src[:, P // 2 :])
+        nc.vector.tensor_copy(dst[:, :EARLY_WORDS, 2:], src[:, :EARLY_WORDS, 2:])
+        nc.vector.tensor_copy(dst[:, EARLY_WORDS : P - LATE_WORDS], src[:, EARLY_WORDS : P - LATE_WORDS])
+        nc.scalar.activation(dst[:, P - LATE_WORDS :], src[:, P - LATE_WORDS :], ACT.Copy)
         for u in range(2):
             cols = slice(2 * u * P, 2 * (u + 1) * P)
             nc.vector.quantize_mx(out=w_codes[:, cols].bitcast(FP8X4), scales=w_plane[:, cols], in_=w_grouped[u][:].rearrange("p e m j -> p (e m j)"))

@@ -85,10 +85,10 @@ def tile_picked_phrank_none_po_kernel(tc, x_words, x_scales, w1, prior, offs, ou
         for h in range(2):
             nc.vector.tensor_copy(x_codes[h][:], word_table[:].bitcast(U32).indirect(offsets[:, h * HALF // 16 : (h + 1) * HALF // 16]))
 
-        logits = [keep.tile([P, S], F32, name=f"logits{t}", align_bytes=64) for t in range(PACK)]
+        logits = [keep.tile([P, S], F32, name=f"logits{t}", tag=f"logits{t}", align_bytes=64) for t in range(PACK)]
         staged = keep.tile([P, S], F32, name="staged", align_bytes=64)
         expd = [keep.tile([P, S], F32, name=f"expd{t}", align_bytes=64) for t in range(PACK)]
-        neg_max = [keep.tile([P, 1], F32, name=f"neg_max{t}") for t in range(PACK)]
+        neg_max = [keep.tile([P, 1], F32, name=f"neg_max{t}", tag={3: "neg_max0", 1: "logits0"}.get(t, f"neg_max{t}"), align_bytes=64) for t in range(PACK)]
         total = [keep.tile([P, 1], F32, name=f"total{t}") for t in range(PACK)]
         inv = [keep.tile([P, 1], F32, name=f"inv{t}") for t in range(PACK)]
         probs = keep.tile([P, PACK, S], F32, name="probs", align_bytes=64)

from contextlib import ExitStack

import concourse.mybir as mybir

K, T, S, N = 512, 2048, 512, 512
FLOPS = 2 * K * S * N

F32 = mybir.dt.float32
BF16 = mybir.dt.bfloat16
I32 = mybir.dt.int32
U32 = mybir.dt.uint32
U16 = mybir.dt.uint16
U8 = mybir.dt.uint8
FP8X4 = mybir.dt.float8_e4m3fn_x4
ALU = mybir.AluOpType
ACT = mybir.ActivationFunctionType
AX = mybir.AxisListType

P = 128
PACK = 4
QUAD = 32
BLOCK_PARTS = 8
HALF = S // 2
QUARTER = S // 4
W_LEAD = N + N // 2
EARLY_WORDS = 16
LATE_WORDS = 32
VECTOR_COLS = 352


def tile_picked_phrank_none_po_kernel(tc, x_words, x_scales, w1, prior, offs, out_0, out_1, out_2):
    nc = tc.nc
    with ExitStack() as ctx:
        keep = ctx.enter_context(tc.tile_pool(name="keep", bufs=1))
        psum = ctx.enter_context(tc.psum_pool(name="psum", bufs=1))

        offsets = keep.tile([P, S // 16], U16, name="offsets")
        scale_table = keep.tile([P, T], U8, name="scale_table", tag="table_then_prior", align_bytes=64)
        word_table = keep.tile([P, T], I32, name="word_table", align_bytes=64)
        w_raw = keep.tile([P, PACK, N], F32, name="w_raw", align_bytes=64)

        nc.vector.memset(scale_table[:].bitcast(I32), 0)
        x_plane = keep.tile([P, S], U8, name="x_plane", align_bytes=64)
        nc.vector.memset(x_plane[:].bitcast(I32), 0)

        table_rows = x_words[0].rearrange("p n t -> p (n t)").bitcast(I32)
        w_flat = w_raw[:].rearrange("p j m -> p (j m)")
        w_runs = w1.rearrange("(p j) m -> p (j m)", j=PACK)
        nc.sync.dma_start(out=w_flat[:, :W_LEAD], in_=w_runs[:, :W_LEAD])
        nc.sync.dma_start(offsets[:], offs)
        nc.sync.dma_start(out=scale_table[:].bitcast(I32)[0:P:BLOCK_PARTS, :], in_=x_scales[0].bitcast(I32))
        nc.sync.dma_start(out=w_flat[:, W_LEAD:], in_=w_runs[:, W_LEAD:])
        nc.sync.dma_start(out=word_table[:], in_=table_rows)

        picked_scales = keep.tile([P, S], U8, name="picked_scales", align_bytes=64)
        nc.vector.tensor_copy(picked_scales[:], scale_table[:].indirect(offsets[:]))
        for r in range(4):
            nc.scalar.dma_start(out=x_plane[:].bitcast(I32)[r:P:QUAD, :], in_=picked_scales[:].bitcast(I32)[BLOCK_PARTS * r : P : QUAD, :])
        prior_sb = keep.tile([P, S], F32, name="prior_sb", tag="table_then_prior", align_bytes=64)
        for lo in (0, HALF):
            nc.sync.dma_start(out=prior_sb[:, lo : lo + HALF], in_=prior[:, lo : lo + HALF])

        w_codes = keep.tile([P, N], U32, name="w_codes", align_bytes=64)
        w_plane = keep.tile([P, N], U8, name="w_plane", align_bytes=64)
        w_grouped = [keep.tile([P, 2, P, PACK], BF16, name=f"w_grouped{u}", align_bytes=64) for u in range(2)]

        def w_views(u):
            dst = w_grouped[u][:].rearrange("p e m j -> p m j e")
            src = w_raw[:].rearrange("p j (m u e) -> p u m j e", u=2, e=2)[:, u]
            return dst, src

        dst, src = w_views(1)
        nc.scalar.activation(dst[:, :EARLY_WORDS, :2], src[:, :EARLY_WORDS, :2], ACT.Copy)
        nc.vector.tensor_copy(*w_views(0))
        nc.vector.tensor_copy(dst[:, :EARLY_WORDS, 2:], src[:, :EARLY_WORDS, 2:])
        nc.vector.tensor_copy(dst[:, EARLY_WORDS : P - LATE_WORDS], src[:, EARLY_WORDS : P - LATE_WORDS])
        nc.scalar.activation(dst[:, P - LATE_WORDS :], src[:, P - LATE_WORDS :], ACT.Copy)
        for u in range(2):
            cols = slice(2 * u * P, 2 * (u + 1) * P)
            nc.vector.quantize_mx(out=w_codes[:, cols].bitcast(FP8X4), scales=w_plane[:, cols], in_=w_grouped[u][:].rearrange("p e m j -> p (e m j)"))

        halves = [slice(0, HALF), slice(HALF, S)]
        whole = slice(0, S)
        x_codes = [keep.tile([P, HALF], U32, name=f"x_codes{h}", align_bytes=64) for h in range(2)]
        for h in range(2):
            nc.vector.tensor_copy(x_codes[h][:], word_table[:].bitcast(U32).indirect(offsets[:, h * HALF // 16 : (h + 1) * HALF // 16]))

        logits = [keep.tile([P, S], F32, name=f"logits{t}", tag=f"logits{t}", align_bytes=64) for t in range(PACK)]
        staged = keep.tile([P, S], F32, name="staged", align_bytes=64)
        expd = [keep.tile([P, S], F32, name=f"expd{t}", align_bytes=64) for t in range(PACK)]
        neg_max = [keep.tile([P, 1], F32, name=f"neg_max{t}", tag={3: "neg_max0", 1: "logits0"}.get(t, f"neg_max{t}"), align_bytes=64) for t in range(PACK)]
        total = [keep.tile([P, 1], F32, name=f"total{t}") for t in range(PACK)]
        inv = [keep.tile([P, 1], F32, name=f"inv{t}") for t in range(PACK)]
        probs = keep.tile([P, PACK, S], F32, name="probs", align_bytes=64)
        out_rows = out_0.rearrange("(p t) c -> p t c", t=PACK)

        def scores(t, h):
            bank = psum.tile([P, HALF], F32, name=f"bank{t}_{h}")
            nc.tensor.matmul_mx(
                out=bank[:],
                lhsT=w_codes[:, t * P : (t + 1) * P].bitcast(FP8X4),
                lhsT_scale=w_plane[:, t * P : (t + 1) * P],
                rhs=x_codes[h][:].bitcast(FP8X4),
                rhs_scale=x_plane[:, halves[h]],
                start=True,
                stop=True,
            )
            return bank

        def add_prior(t, h):
            cols = halves[h]
            nc.vector.tensor_tensor(logits[t][:, cols], scores(t, h)[:], prior_sb[:, cols], ALU.add)

        def add_prior_off_vector(t, h):
            cols = halves[h]
            nc.scalar.copy(staged[:, cols], scores(t, h)[:])
            nc.gpsimd.tensor_tensor(logits[t][:, cols], staged[:, cols], prior_sb[:, cols], ALU.add)

        def exponentiate(t):
            nc.vector.tensor_reduce(neg_max[t][:], logits[t][:], AX.X, ALU.max, negate=True)
            nc.scalar.activation(expd[t][:], logits[t][:], ACT.Exp, bias=neg_max[t][:], accum_out=total[t][:])

        def scale_on_scalar(t, cols):
            nc.scalar.activation(probs[:, t, cols], expd[t][:, cols], ACT.Copy, scale=inv[t][:])

        def scale_on_vector(t, cols):
            nc.vector.tensor_scalar(probs[:, t, cols], expd[t][:, cols], inv[t][:], None, ALU.mult)

        def store_rows(t):
            nc.sync.dma_start(out=out_rows[:, t, :], in_=probs[:, t, :])

        for h in range(2):
            add_prior(0, h)
            add_prior(2, h)
        for h in range(2):
            add_prior_off_vector(1, h)
        exponentiate(0)
        for h in range(2):
            add_prior(3, h)
        exponentiate(2)
        nc.vector.reciprocal(inv[0][:], total[0][:])
        nc.gpsimd.tensor_scalar(probs[:, 0, :], expd[0][:], inv[0][:], 0.0, ALU.mult, ALU.add)
        store_rows(0)
        for t in (3, 1):
            exponentiate(t)
        for t in (2, 3):
            nc.vector.reciprocal(inv[t][:], total[t][:])
        for t in (2, 3):
            scale_on_vector(t, whole)
            store_rows(t)
        nc.vector.reciprocal(inv[1][:], total[1][:])
        scale_on_scalar(1, slice(VECTOR_COLS, S))
        scale_on_vector(1, slice(0, QUARTER))
        scale_on_vector(1, slice(QUARTER, VECTOR_COLS))
        store_rows(1)

        y_grouped = keep.tile([P, S, PACK], BF16, name="y_grouped", align_bytes=64)
        y_dst = y_grouped[:].rearrange("p (c i) t -> p c t i", i=4)
        y_src = probs[:].rearrange("p t (c i) -> p c t i", i=4)
        y_codes = keep.tile([P, S], U32, name="y_codes", align_bytes=64)
        y_plane = keep.tile([P, S], U8, name="y_plane", align_bytes=64)
        nc.scalar.copy(out=y_dst[:, VECTOR_COLS // 4 :], in_=y_src[:, VECTOR_COLS // 4 :])
        for lo, hi in ((0, QUARTER), (QUARTER, HALF), (HALF, VECTOR_COLS)):
            nc.vector.tensor_copy(out=y_dst[:, lo // 4 : hi // 4], in_=y_src[:, lo // 4 : hi // 4])
        words_out = out_1[0].rearrange("p n t -> p (n t)").bitcast(I32)
        for cols in (slice(0, QUARTER), slice(QUARTER, HALF), halves[1]):
            nc.vector.quantize_mx(out=y_codes[:, cols].bitcast(FP8X4), scales=y_plane[:, cols], in_=y_grouped[:, cols, :].rearrange("p c t -> p (c t)"))
        for cols in halves:
            nc.sync.dma_start(out=words_out[:, cols], in_=y_codes[:, cols].bitcast(I32))
        for q in range(4):
            queue = nc.scalar if q < 2 else nc.sync
            queue.dma_start(out=out_2[0].bitcast(I32)[4 * q : 4 * q + 4, :], in_=y_plane[:].bitcast(I32)[QUAD * q : QUAD * q + 4, :])
